import numpy as np
import ml_dtypes


def mxq(x, axis, fmt="e4m3"):
    dtype, down = {"e4m3": (ml_dtypes.float8_e4m3fn, 7), "e5m2": (ml_dtypes.float8_e5m2, 14)}[fmt]
    v = np.moveaxis(np.asarray(x, np.float32).astype(ml_dtypes.bfloat16).astype(np.float64), axis, -1)
    blocks = v.reshape(v.shape[:-1] + (-1, 32))
    amax = np.abs(blocks).max(-1, keepdims=True)
    byte = np.maximum(np.where(amax > 0, np.frexp(amax)[1] - 1 + 127, 0) - down, 1)
    scale = np.exp2(byte - 127.0)
    codes = (blocks / scale).astype(np.float32).astype(dtype).astype(np.float64)
    return np.moveaxis((codes * scale).reshape(v.shape), -1, axis)


WIDE = False


def mx_kscale(k):
    if not WIDE:
        return np.ones(k)
    levels = np.array([10, -10, 5, -5, 0])
    if k % 512:
        return np.exp2(np.random.permutation(np.resize(levels, k // 32))).repeat(32)
    a = np.empty((k // 512, 16))
    for p in range(k // 512):
        a[p, :8] = np.random.permutation(np.resize(levels, 8))
        for g in range(8):
            far = levels[np.abs(levels - a[p, g]) >= 10]
            a[p, g + 8] = far[np.random.randint(len(far))]
    return np.exp2(a.ravel()).repeat(32)


def f64(x):
    return np.asarray(x).astype(np.float64)


def striped(idx):
    return np.tile(idx.reshape(-1, 16).T, (8, 1)).astype(np.uint16)


def unstriped(offs):
    return offs[:16].T.reshape(-1).astype(np.int64)


def striped8(idx):
    return np.concatenate([x.reshape(-1, 16).T for x in idx]).astype(np.uint16)


def runs(offs, k):
    lists = np.stack([offs[16 * r : 16 * r + 16].T.reshape(-1) for r in range(8)]).astype(np.int64)
    return lists[np.arange(k) % 512 // 64]


def pack_weight(w):
    k, n = w.shape
    w = f64(np.asarray(w, np.float32).astype(ml_dtypes.bfloat16)).reshape(k // 32, 32, n)
    amax = np.abs(w).max(1)
    byte = np.clip(np.where(amax > 0, np.frexp(amax)[1] - 1 + 127 - 7, 1), 1, 254)
    scaled = (w * np.exp2(127.0 - byte)[:, None, :]).reshape(k, n).astype(np.float32)
    words = np.ascontiguousarray(scaled.reshape(k // 512, 128, 4, n).transpose(0, 1, 3, 2)).astype(ml_dtypes.float8_e4m3fn).view(np.uint8)
    return words, np.ascontiguousarray(byte.astype(np.uint8).reshape(k // 512, 16, n))


def unpack_weight(words, scales):
    g, p, n, _ = words.shape
    vals = np.ascontiguousarray(words).view(ml_dtypes.float8_e4m3fn).astype(np.float64) * np.repeat(np.exp2(scales.astype(np.float64) - 127.0), 8, axis=1)[..., None]
    return vals.transpose(0, 1, 3, 2).reshape(g * 512, n)

def planes(y):
    n, m = y.shape
    v = y.astype(np.float32).astype(ml_dtypes.bfloat16).astype(np.float64).reshape(n // 32, 32, m)
    top = np.abs(v).max(1)
    byte = np.clip(np.where(top > 0, np.frexp(top)[1] - 1 + 127 - 7, 1), 1, 254)
    codes = (v * np.exp2(127.0 - byte)[:, None, :]).reshape(n, m).astype(np.float32).astype(ml_dtypes.float8_e4m3fn).view(np.uint8)
    words = codes.reshape(n // 512, 128, 4, m).transpose(0, 1, 3, 2)
    return np.ascontiguousarray(words), np.ascontiguousarray(byte.astype(np.uint8).reshape(n // 512, 16, m))


K, T, S, V, N, H = 512, 2048, 1024, 512, 512, 512


def setup_inputs():
    n = np.random.standard_normal
    s = mx_kscale(K)[:, None]
    u = mx_kscale(H)
    packed_xT = pack_weight(n((K, T)) * s)
    packed_w1 = pack_weight(n((K, H)) / np.sqrt(K) / s)
    packed_w2 = pack_weight(n((H, N)) / np.sqrt(H) / u[:, None])
    return {
        "x_words": packed_xT[0],
        "x_scales": packed_xT[1],
        "w1_words": packed_w1[0],
        "w1_scales": packed_w1[1],
        "gn": (np.random.uniform(0.5, 1.5, (H, 1)) * u[:, None]).astype(np.float32),
        "w2_words": packed_w2[0],
        "w2_scales": packed_w2[1],
        "offs": striped(np.random.permutation(T)[:S]),
        "order": striped8(np.stack([np.random.permutation(S) for _ in range(8)])),
        "n1": striped8(np.stack([np.random.permutation(V) for _ in range(8)])),
        "n2": striped8(np.stack([np.random.permutation(V) for _ in range(8)])),
    }


def reference(x_words, x_scales, w1_words, w1_scales, gn, w2_words, w2_scales, offs, order, n1, n2):
    xq = unpack_weight(x_words, x_scales)[:, unstriped(offs)]
    y = unpack_weight(w1_words, w1_scales).T @ xq
    o = y[np.arange(H)[:, None], runs(order, H)]
    mx = o.reshape(H, V, 2).max(axis=2)
    mn = o.reshape(H, V, 2).min(axis=2)
    z = f64(gn) * (mx * np.tanh(mn))
    h = unpack_weight(w2_words, w2_scales).T @ mxq(z, 0, "e4m3")
    out_0 = h - (0.5 * (h[np.arange(N)[:, None], runs(n1, N)] + h[np.arange(N)[:, None], runs(n2, N)]))
    return (out_0,) + planes(out_0)

@@ -1,0 +1,237 @@
+from contextlib import ExitStack
+
+import concourse.mybir as mybir
+
+K, T, S, V, N, H = 512, 2048, 1024, 512, 512, 512
+FLOPS = 2 * K * H * S + 2 * H * N * V
+
+F32 = mybir.dt.float32
+BF16 = mybir.dt.bfloat16
+I32 = mybir.dt.int32
+U32 = mybir.dt.uint32
+U16 = mybir.dt.uint16
+U8 = mybir.dt.uint8
+FP8X4 = mybir.dt.float8_e4m3fn_x4
+ALU = mybir.AluOpType
+ACT = mybir.ActivationFunctionType
+
+P = 128
+PACK = 4
+STRIPE = 16
+QUADS = 4
+BANK = 512
+
+TOKEN_PIECES = (512, 256, 256)
+POOL_PIECES = (256, 128, 128)
+OUT_PIECES = (256, 128, 128)
+
+
+def spans(widths):
+    starts = [sum(widths[:i]) for i in range(len(widths))]
+    return list(zip(starts, widths))
+
+
+def entries(list_tile, start, count):
+    return list_tile[:, start // STRIPE : (start + count) // STRIPE]
+
+
+def words_of(dram):
+    return dram[0].rearrange("p n t -> p (n t)").bitcast(I32)
+
+
+def load_scale_rows(queue, plane, dram):
+    rows = dram[0].bitcast(I32)
+    for q in range(QUADS):
+        queue.dma_start(plane[32 * q : 32 * q + 4, :].bitcast(I32), rows[4 * q : 4 * q + 4, :])
+
+
+def by_plane(flat):
+    return flat.rearrange("p (t c i) -> p c t i", t=PACK, i=2)
+
+
+def by_column(flat):
+    return flat.rearrange("p (c i t) -> p c t i", t=PACK, i=2)
+
+
+def tile_picked_prodpool_none_po_kernel(
+    tc, x_words, x_scales, w1_words, w1_scales, gn, w2_words, w2_scales, offs, order, n1, n2, out_0, out_1, out_2
+):
+    nc = tc.nc
+    with ExitStack() as ctx:
+        keep = ctx.enter_context(tc.tile_pool(name="keep", bufs=1))
+        psum = ctx.enter_context(tc.psum_pool(name="psum", bufs=8))
+
+        def sbuf(name, shape, dtype):
+            return keep.tile(shape, dtype, name=name, align_bytes=64)
+
+        offs_sb = sbuf("offs_sb", [P, S // STRIPE], U16)
+        order_sb = sbuf("order_sb", [P, S // STRIPE], U16)
+        n1_sb = sbuf("n1_sb", [P, V // STRIPE], U16)
+        n2_sb = sbuf("n2_sb", [P, V // STRIPE], U16)
+        x_table = sbuf("x_table", [P, T], U32)
+        x_plane = sbuf("x_plane", [P, T], U8)
+        w1_raw = sbuf("w1_raw", [P, H], I32)
+        w2_raw = sbuf("w2_raw", [P, N], I32)
+        w1_raw_plane = sbuf("w1_raw_plane", [P, H], U8)
+        w2_raw_plane = sbuf("w2_raw_plane", [P, N], U8)
+        gain = sbuf("gain", [P, PACK], F32)
+
+        nc.vector.memset(x_plane[:].bitcast(I32), 0)
+        nc.gpsimd.memset(w1_raw_plane[:].bitcast(I32), 0)
+        nc.gpsimd.memset(w2_raw_plane[:].bitcast(I32), 0)
+
+        nc.sync.dma_start(offs_sb[:], offs)
+        nc.sync.dma_start(w1_raw[:], words_of(w1_words))
+        load_scale_rows(nc.sync, x_plane, x_scales)
+        nc.sync.dma_start(x_table[:].bitcast(I32), words_of(x_words))
+        nc.sync.dma_start(gain[:], gn.rearrange("(p t) o -> p (t o)", t=PACK))
+        load_scale_rows(nc.sync, w1_raw_plane, w1_scales)
+        nc.sync.dma_start(order_sb[:], order)
+        nc.sync.dma_start(w2_raw[:], words_of(w2_words))
+        load_scale_rows(nc.sync, w2_raw_plane, w2_scales)
+        nc.sync.dma_start(n1_sb[:], n1)
+        nc.sync.dma_start(n2_sb[:], n2)
+
+        warm = sbuf("warm", [P, PACK], F32)
+        nc.scalar.activation(warm[:], gain[:], ACT.Tanh)
+
+        def deal_words(name, raw):
+            dealt = sbuf(name, [P, PACK * P], U32)
+            nc.vector.tensor_copy(
+                dealt[:].bitcast(I32).rearrange("p (t c i) -> p c t i", t=PACK, i=4),
+                raw[:].rearrange("p (c i t) -> p c t i", t=PACK, i=4),
+            )
+            return dealt
+
+        def deal_plane(name, raw):
+            dealt = sbuf(name, [P, PACK * P], U8)
+            nc.vector.tensor_copy(
+                dealt[:].rearrange("p (t m) -> p t m", t=PACK), raw[:].rearrange("p (m t) -> p t m", t=PACK)
+            )
+            return dealt
+
+        def product(w_codes, w_plane, codes, plane, width):
+            per_bank = BANK // width
+            results = []
+            for t in range(PACK):
+                if t % per_bank == 0:
+                    bank = psum.tile([P, BANK], F32, name="bank")
+                result = bank[:, (t % per_bank) * width : (t % per_bank + 1) * width]
+                nc.tensor.matmul_mx(
+                    out=result,
+                    lhsT=w_codes[:, t * P : (t + 1) * P].bitcast(FP8X4),
+                    lhsT_scale=w_plane[:, t * P : (t + 1) * P],
+                    rhs=codes.bitcast(FP8X4),
+                    rhs_scale=plane,
+                    start=True,
+                    stop=True,
+                )
+                results.append(result)
+            return results
+
+        w1_codes = deal_words("w1_codes", w1_raw)
+        picked_plane = sbuf("picked_plane", [P, S], U8)
+        nc.vector.tensor_copy(picked_plane[:], x_plane[:].indirect(offs_sb[:]))
+        w1_plane = deal_plane("w1_plane", w1_raw_plane)
+        y = [sbuf("y%d" % t, [P, S], F32) for t in range(PACK)]
+        y_psum = []
+        for start, width in spans(TOKEN_PIECES):
+            picked = sbuf("picked%d" % start, [P, width], U32)
+            nc.vector.tensor_copy(picked[:], x_table[:].indirect(entries(offs_sb, start, width)))
+            y_psum.append(product(w1_codes, w1_plane, picked[:], picked_plane[:, start : start + width], width))
+        for t in range(PACK):
+            for (start, width), results in zip(spans(TOKEN_PIECES), y_psum):
+                nc.scalar.copy(y[t][:, start : start + width], results[t])
+        w2_codes = deal_words("w2_codes", w2_raw)
+        w2_plane = deal_plane("w2_plane", w2_raw_plane)
+
+        half_h = [sbuf("half_h%d" % t, [P, V], F32) for t in range(PACK)]
+        h = sbuf("h", [P, PACK, V], F32)
+
+        def line_up(start, width):
+            lined = sbuf("lined%d" % start, [P, PACK * 2 * width], F32)
+            for t in range(PACK):
+                nc.vector.tensor_copy(
+                    lined[:, t * 2 * width : (t + 1) * 2 * width],
+                    y[t][:].indirect(entries(order_sb, 2 * start, 2 * width)),
+                )
+            smaller = sbuf("smaller%d" % start, [P, PACK * width], F32)
+            larger = sbuf("larger%d" % start, [P, PACK * width], F32)
+            nc.vector.tensor_tensor(smaller[:], lined[:, 0::2], lined[:, 1::2], ALU.min)
+            nc.vector.tensor_tensor(larger[:], lined[:, 0::2], lined[:, 1::2], ALU.max)
+            bent = sbuf("bent%d" % start, [P, PACK * width], F32)
+            nc.scalar.activation(bent[:], smaller[:], ACT.Tanh)
+            gained = sbuf("gained%d" % start, [P, PACK * width], F32)
+            for t in range(PACK):
+                cols = slice(t * width, (t + 1) * width)
+                nc.scalar.activation(gained[:, cols], larger[:, cols], ACT.Copy, scale=gain[:, t : t + 1])
+            return gained, bent
+
+        def second_product(start, width, gained, bent):
+            z = sbuf("z%d" % start, [P, width * PACK], BF16)
+            nc.vector.tensor_tensor(by_column(z[:]), by_plane(gained[:]), by_plane(bent[:]), ALU.mult)
+            z_codes = sbuf("z_codes%d" % start, [P, width], U32)
+            z_plane = sbuf("z_plane%d" % start, [P, width], U8)
+            nc.vector.quantize_mx(out=z_codes[:].bitcast(FP8X4), scales=z_plane[:], in_=z[:])
+            results = product(w2_codes, w2_plane, z_codes[:], z_plane[:], width)
+            for t in range(PACK):
+                nc.scalar.mul(half_h[t][:, start : start + width], results[t], -0.5)
+            for t in range(PACK):
+                nc.scalar.copy(h[:, t, start : start + width], results[t])
+
+        waiting = None
+        for start, width in spans(POOL_PIECES):
+            pooled = line_up(start, width)
+            if waiting is not None:
+                second_product(*waiting)
+            waiting = (start, width) + pooled
+        second_product(*waiting)
+
+        out_rows = out_0.rearrange("(p t) v -> p t v", t=PACK)
+        out_words = words_of(out_1)
+        out_plane = sbuf("out_plane", [P, V], U8)
+
+        def neighbours(start, width):
+            partial = sbuf("partial%d" % start, [P, PACK * width], F32)
+            result = sbuf("result%d" % start, [P, PACK * width], F32)
+            for pair in range(0, PACK, 2):
+                for t in (pair, pair + 1):
+                    nc.vector.tensor_tensor(
+                        partial[:, t * width : (t + 1) * width],
+                        half_h[t][:].indirect(entries(n1_sb, start, width)),
+                        h[:, t, start : start + width],
+                        ALU.add,
+                    )
+                for t in (pair, pair + 1):
+                    nc.vector.tensor_tensor(
+                        result[:, t * width : (t + 1) * width],
+                        half_h[t][:].indirect(entries(n2_sb, start, width)),
+                        partial[:, t * width : (t + 1) * width],
+                        ALU.add,
+                    )
+            nc.sync.dma_start(out_rows[:, :, start : start + width], result[:].rearrange("p (t v) -> p t v", t=PACK))
+            rounded = sbuf("rounded%d" % start, [P, width * PACK], BF16)
+            if start + width < V:
+                nc.scalar.copy(by_column(rounded[:]), by_plane(result[:]))
+            else:
+                nc.vector.tensor_copy(by_column(rounded[:]), by_plane(result[:]))
+            return rounded
+
+        def planes(start, width, rounded):
+            codes = sbuf("codes%d" % start, [P, width], U32)
+            nc.vector.quantize_mx(
+                out=codes[:].bitcast(FP8X4), scales=out_plane[:, start : start + width], in_=rounded[:]
+            )
+            nc.sync.dma_start(out_words[:, start : start + width], codes[:].bitcast(I32))
+
+        waiting = None
+        for start, width in spans(OUT_PIECES):
+            rounded = neighbours(start, width)
+            if waiting is not None:
+                planes(*waiting)
+            waiting = (start, width, rounded)
+        planes(*waiting)
+        scale_rows = out_2[0].bitcast(I32)
+        for q in range(QUADS):
+            queue = nc.scalar if q % 2 else nc.sync
+            queue.dma_start(scale_rows[4 * q : 4 * q + 4, :], out_plane[32 * q : 32 * q + 4, :].bitcast(I32))

@@ -49,6 +49,10 @@ def by_plane(flat):
     return flat.rearrange("p (t c i) -> p c t i", t=PACK, i=2)
 
 
+def in_pairs(planes):
+    return planes.rearrange("p t (c i) -> p c t i", i=2)
+
+
 def by_column(flat):
     return flat.rearrange("p (c i t) -> p c t i", t=PACK, i=2)
 
@@ -61,8 +65,8 @@ def tile_picked_prodpool_none_po_kernel(
         keep = ctx.enter_context(tc.tile_pool(name="keep", bufs=1))
         psum = ctx.enter_context(tc.psum_pool(name="psum", bufs=8))
 
-        def sbuf(name, shape, dtype):
-            return keep.tile(shape, dtype, name=name, align_bytes=64)
+        def sbuf(name, shape, dtype, tag=""):
+            return keep.tile(shape, dtype, name=name, tag=tag or name, align_bytes=64)
 
         offs_sb = sbuf("offs_sb", [P, S // STRIPE], U16)
         order_sb = sbuf("order_sb", [P, S // STRIPE], U16)
@@ -72,7 +76,7 @@ def tile_picked_prodpool_none_po_kernel(
         x_plane = sbuf("x_plane", [P, T], U8)
         w1_raw = sbuf("w1_raw", [P, H], I32)
         w2_raw = sbuf("w2_raw", [P, N], I32)
-        w1_raw_plane = sbuf("w1_raw_plane", [P, H], U8)
+        w1_raw_plane = sbuf("w1_raw_plane", [P, H], U8, "w1_raw_plane")
         w2_raw_plane = sbuf("w2_raw_plane", [P, N], U8)
         gain = sbuf("gain", [P, PACK], F32)
 
@@ -84,16 +88,13 @@ def tile_picked_prodpool_none_po_kernel(
         nc.sync.dma_start(w1_raw[:], words_of(w1_words))
         load_scale_rows(nc.sync, x_plane, x_scales)
         nc.sync.dma_start(x_table[:].bitcast(I32), words_of(x_words))
-        nc.sync.dma_start(gain[:], gn.rearrange("(p t) o -> p (t o)", t=PACK))
         load_scale_rows(nc.sync, w1_raw_plane, w1_scales)
         nc.sync.dma_start(order_sb[:], order)
+        nc.sync.dma_start(gain[:], gn.rearrange("(p t) o -> p (t o)", t=PACK))
         nc.sync.dma_start(w2_raw[:], words_of(w2_words))
         load_scale_rows(nc.sync, w2_raw_plane, w2_scales)
         nc.sync.dma_start(n1_sb[:], n1)
         nc.sync.dma_start(n2_sb[:], n2)
-
-        warm = sbuf("warm", [P, PACK], F32)
-        nc.scalar.activation(warm[:], gain[:], ACT.Tanh)
 
         def deal_words(name, raw):
             dealt = sbuf(name, [P, PACK * P], U32)
@@ -110,6 +111,17 @@ def tile_picked_prodpool_none_po_kernel(
             )
             return dealt
 
+        def multiply_mx(result, w_codes, w_plane, t, codes, plane):
+            nc.tensor.matmul_mx(
+                out=result,
+                lhsT=w_codes[:, t * P : (t + 1) * P].bitcast(FP8X4),
+                lhsT_scale=w_plane[:, t * P : (t + 1) * P],
+                rhs=codes.bitcast(FP8X4),
+                rhs_scale=plane,
+                start=True,
+                stop=True,
+            )
+
         def product(w_codes, w_plane, codes, plane, width):
             per_bank = BANK // width
             results = []
@@ -117,82 +129,92 @@ def tile_picked_prodpool_none_po_kernel(
                 if t % per_bank == 0:
                     bank = psum.tile([P, BANK], F32, name="bank")
                 result = bank[:, (t % per_bank) * width : (t % per_bank + 1) * width]
-                nc.tensor.matmul_mx(
-                    out=result,
-                    lhsT=w_codes[:, t * P : (t + 1) * P].bitcast(FP8X4),
-                    lhsT_scale=w_plane[:, t * P : (t + 1) * P],
-                    rhs=codes.bitcast(FP8X4),
-                    rhs_scale=plane,
-                    start=True,
-                    stop=True,
-                )
+                multiply_mx(result, w_codes, w_plane, t, codes, plane)
                 results.append(result)
             return results
 
         w1_codes = deal_words("w1_codes", w1_raw)
         picked_plane = sbuf("picked_plane", [P, S], U8)
         nc.vector.tensor_copy(picked_plane[:], x_plane[:].indirect(offs_sb[:]))
-        w1_plane = deal_plane("w1_plane", w1_raw_plane)
-        y = [sbuf("y%d" % t, [P, S], F32) for t in range(PACK)]
-        y_psum = []
+        picked = []
         for start, width in spans(TOKEN_PIECES):
-            picked = sbuf("picked%d" % start, [P, width], U32)
-            nc.vector.tensor_copy(picked[:], x_table[:].indirect(entries(offs_sb, start, width)))
-            y_psum.append(product(w1_codes, w1_plane, picked[:], picked_plane[:, start : start + width], width))
+            piece = sbuf("picked%d" % start, [P, width], U32, "w1_raw_plane" if start == TOKEN_PIECES[0] else "")
+            nc.vector.tensor_copy(piece[:], x_table[:].indirect(entries(offs_sb, start, width)))
+            picked.append(piece)
+            if start == 0:
+                w1_plane = deal_plane("w1_plane", w1_raw_plane)
+        y = [sbuf("y%d" % t, [P, S], F32) for t in range(PACK)]
         for t in range(PACK):
-            for (start, width), results in zip(spans(TOKEN_PIECES), y_psum):
-                nc.scalar.copy(y[t][:, start : start + width], results[t])
+            for (start, width), piece in zip(spans(TOKEN_PIECES), picked):
+                bank = psum.tile([P, BANK], F32, name="bank")
+                multiply_mx(bank[:, :width], w1_codes, w1_plane, t, piece[:], picked_plane[:, start : start + width])
+                nc.scalar.copy(y[t][:, start : start + width], bank[:, :width])
         w2_codes = deal_words("w2_codes", w2_raw)
         w2_plane = deal_plane("w2_plane", w2_raw_plane)
 
         half_h = [sbuf("half_h%d" % t, [P, V], F32) for t in range(PACK)]
         h = sbuf("h", [P, PACK, V], F32)
 
-        def line_up(start, width):
-            lined = sbuf("lined%d" % start, [P, PACK * 2 * width], F32)
-            for t in range(PACK):
+        lined = sbuf("lined", [P, PACK, S], F32)
+        smaller = sbuf("smaller", [P, PACK, V], F32)
+        larger = sbuf("larger", [P, PACK, V], F32)
+        bent = sbuf("bent", [P, PACK, V], F32)
+        gained = sbuf("gained", [P, PACK, V], F32)
+        halves = [slice(0, V // 2), slice(V // 2, V)]
+        for t in range(PACK):
+            for half in halves:
                 nc.vector.tensor_copy(
-                    lined[:, t * 2 * width : (t + 1) * 2 * width],
-                    y[t][:].indirect(entries(order_sb, 2 * start, 2 * width)),
+                    lined[:, t, 2 * half.start : 2 * half.stop],
+                    y[t][:].indirect(entries(order_sb, 2 * half.start, V)),
                 )
-            smaller = sbuf("smaller%d" % start, [P, PACK * width], F32)
-            larger = sbuf("larger%d" % start, [P, PACK * width], F32)
-            nc.vector.tensor_tensor(smaller[:], lined[:, 0::2], lined[:, 1::2], ALU.min)
-            nc.vector.tensor_tensor(larger[:], lined[:, 0::2], lined[:, 1::2], ALU.max)
-            bent = sbuf("bent%d" % start, [P, PACK * width], F32)
-            nc.scalar.activation(bent[:], smaller[:], ACT.Tanh)
-            gained = sbuf("gained%d" % start, [P, PACK * width], F32)
-            for t in range(PACK):
-                cols = slice(t * width, (t + 1) * width)
-                nc.scalar.activation(gained[:, cols], larger[:, cols], ACT.Copy, scale=gain[:, t : t + 1])
-            return gained, bent
+            for half in halves:
+                first = lined[:, t, 2 * half.start : 2 * half.stop : 2]
+                second = lined[:, t, 2 * half.start + 1 : 2 * half.stop : 2]
+                nc.vector.tensor_tensor(smaller[:, t, half], first, second, ALU.min)
+                nc.vector.tensor_tensor(larger[:, t, half], first, second, ALU.max)
+                nc.scalar.activation(bent[:, t, half], smaller[:, t, half], ACT.Tanh)
+                nc.scalar.activation(gained[:, t, half], larger[:, t, half], ACT.Copy, scale=gain[:, t : t + 1])
 
-        def second_product(start, width, gained, bent):
+        def multiply(start, width):
+            cols = slice(start, start + width)
             z = sbuf("z%d" % start, [P, width * PACK], BF16)
-            nc.vector.tensor_tensor(by_column(z[:]), by_plane(gained[:]), by_plane(bent[:]), ALU.mult)
+            nc.vector.tensor_tensor(by_column(z[:]), in_pairs(gained[:, :, cols]), in_pairs(bent[:, :, cols]), ALU.mult)
+            return z
+
+        def second_product(start, width, z):
             z_codes = sbuf("z_codes%d" % start, [P, width], U32)
             z_plane = sbuf("z_plane%d" % start, [P, width], U8)
             nc.vector.quantize_mx(out=z_codes[:].bitcast(FP8X4), scales=z_plane[:], in_=z[:])
-            results = product(w2_codes, w2_plane, z_codes[:], z_plane[:], width)
-            for t in range(PACK):
-                nc.scalar.mul(half_h[t][:, start : start + width], results[t], -0.5)
-            for t in range(PACK):
-                nc.scalar.copy(h[:, t, start : start + width], results[t])
+            return product(w2_codes, w2_plane, z_codes[:], z_plane[:], width)
 
         waiting = None
+        h_psum = []
         for start, width in spans(POOL_PIECES):
-            pooled = line_up(start, width)
+            z = multiply(start, width)
             if waiting is not None:
-                second_product(*waiting)
-            waiting = (start, width) + pooled
-        second_product(*waiting)
+                h_psum.append(second_product(*waiting))
+            waiting = (start, width, z)
+        h_psum.append(second_product(*waiting))
+        pieces = list(zip(spans(POOL_PIECES), h_psum))
+        for t in range(PACK):
+            (start, width), results = pieces[0]
+            nc.scalar.copy(h[:, t, start : start + width], results[t])
+            for (start, width), results in pieces:
+                nc.scalar.mul(half_h[t][:, start : start + width], results[t], -0.5)
+        for (start, width), results in pieces[1:]:
+            for t in range(PACK):
+                nc.scalar.copy(h[:, t, start : start + width], results[t])
 
         out_rows = out_0.rearrange("(p t) v -> p t v", t=PACK)
         out_words = words_of(out_1)
         out_plane = sbuf("out_plane", [P, V], U8)
 
+        def store_rows(start, width, result):
+            nc.sync.dma_start(out_rows[:, :, start : start + width], result.rearrange("p (t v) -> p t v", t=PACK))
+
         def neighbours(start, width):
-            partial = sbuf("partial%d" % start, [P, PACK * width], F32)
+            last = start + width == V
+            partial = sbuf("partial%d" % start, [P, PACK * width], F32, "first_rounded" if last else "")
             result = sbuf("result%d" % start, [P, PACK * width], F32)
             for pair in range(0, PACK, 2):
                 for t in (pair, pair + 1):
@@ -209,12 +231,12 @@ def tile_picked_prodpool_none_po_kernel(
                         partial[:, t * width : (t + 1) * width],
                         ALU.add,
                     )
-            nc.sync.dma_start(out_rows[:, :, start : start + width], result[:].rearrange("p (t v) -> p t v", t=PACK))
-            rounded = sbuf("rounded%d" % start, [P, width * PACK], BF16)
-            if start + width < V:
-                nc.scalar.copy(by_column(rounded[:]), by_plane(result[:]))
-            else:
+            store_rows(start, width, result[:])
+            rounded = sbuf("rounded%d" % start, [P, width * PACK], BF16, "first_rounded" if start == 0 else "")
+            if last:
                 nc.vector.tensor_copy(by_column(rounded[:]), by_plane(result[:]))
+            else:
+                nc.scalar.copy(by_column(rounded[:]), by_plane(result[:]))
             return rounded
 
         def planes(start, width, rounded):

@@ -18,17 +18,12 @@ ACT = mybir.ActivationFunctionType
 P = 128
 PACK = 4
 STRIPE = 16
-QUADS = 4
+QUADRANTS = 4
 BANK = 512
 
-TOKEN_PIECES = (512, 256, 256)
-POOL_PIECES = (256, 128, 128)
-OUT_PIECES = (256, 128, 128)
-
-
-def spans(widths):
-    starts = [sum(widths[:i]) for i in range(len(widths))]
-    return list(zip(starts, widths))
+TOKEN_PIECES = ((0, 512), (512, 256), (768, 256))
+FIRST_HALF, SECOND_HALF = (0, V // 2), (V // 2, V // 2)
+LAST_QUARTERS = ((V // 2, V // 4), (3 * V // 4, V // 4))
 
 
 def entries(list_tile, start, count):
@@ -39,21 +34,17 @@ def words_of(dram):
     return dram[0].rearrange("p n t -> p (n t)").bitcast(I32)
 
 
-def load_scale_rows(queue, plane, dram):
+def load_scale_rows(nc, plane, dram):
     rows = dram[0].bitcast(I32)
-    for q in range(QUADS):
-        queue.dma_start(plane[32 * q : 32 * q + 4, :].bitcast(I32), rows[4 * q : 4 * q + 4, :])
+    for q in range(QUADRANTS):
+        nc.sync.dma_start(plane[32 * q : 32 * q + 4, :].bitcast(I32), rows[4 * q : 4 * q + 4, :])
 
 
-def by_plane(flat):
-    return flat.rearrange("p (t c i) -> p c t i", t=PACK, i=2)
+def from_tiles(values):
+    return values.rearrange("p t (c i) -> p c t i", i=2)
 
 
-def in_pairs(planes):
-    return planes.rearrange("p t (c i) -> p c t i", i=2)
-
-
-def by_column(flat):
+def side_by_side(flat):
     return flat.rearrange("p (c i t) -> p c t i", t=PACK, i=2)
 
 
@@ -65,8 +56,8 @@ def tile_picked_prodpool_none_po_kernel(
         keep = ctx.enter_context(tc.tile_pool(name="keep", bufs=1))
         psum = ctx.enter_context(tc.psum_pool(name="psum", bufs=8))
 
-        def sbuf(name, shape, dtype, tag=""):
-            return keep.tile(shape, dtype, name=name, tag=tag or name, align_bytes=64)
+        def sbuf(name, shape, dtype, reuses=None):
+            return keep.tile(shape, dtype, name=name, tag=reuses or name, align_bytes=64)
 
         offs_sb = sbuf("offs_sb", [P, S // STRIPE], U16)
         order_sb = sbuf("order_sb", [P, S // STRIPE], U16)
@@ -76,7 +67,7 @@ def tile_picked_prodpool_none_po_kernel(
         x_plane = sbuf("x_plane", [P, T], U8)
         w1_raw = sbuf("w1_raw", [P, H], I32)
         w2_raw = sbuf("w2_raw", [P, N], I32)
-        w1_raw_plane = sbuf("w1_raw_plane", [P, H], U8, "w1_raw_plane")
+        w1_raw_plane = sbuf("w1_raw_plane", [P, H], U8)
         w2_raw_plane = sbuf("w2_raw_plane", [P, N], U8)
         gain = sbuf("gain", [P, PACK], F32)
 
@@ -86,13 +77,13 @@ def tile_picked_prodpool_none_po_kernel(
 
         nc.sync.dma_start(offs_sb[:], offs)
         nc.sync.dma_start(w1_raw[:], words_of(w1_words))
-        load_scale_rows(nc.sync, x_plane, x_scales)
+        load_scale_rows(nc, x_plane, x_scales)
         nc.sync.dma_start(x_table[:].bitcast(I32), words_of(x_words))
-        load_scale_rows(nc.sync, w1_raw_plane, w1_scales)
+        load_scale_rows(nc, w1_raw_plane, w1_scales)
         nc.sync.dma_start(order_sb[:], order)
-        nc.sync.dma_start(gain[:], gn.rearrange("(p t) o -> p (t o)", t=PACK))
         nc.sync.dma_start(w2_raw[:], words_of(w2_words))
-        load_scale_rows(nc.sync, w2_raw_plane, w2_scales)
+        load_scale_rows(nc, w2_raw_plane, w2_scales)
+        nc.sync.dma_start(gain[:], gn.rearrange("(p t) o -> p (t o)", t=PACK))
         nc.sync.dma_start(n1_sb[:], n1)
         nc.sync.dma_start(n2_sb[:], n2)
 
@@ -122,138 +113,133 @@ def tile_picked_prodpool_none_po_kernel(
                 stop=True,
             )
 
-        def product(w_codes, w_plane, codes, plane, width):
-            per_bank = BANK // width
-            results = []
-            for t in range(PACK):
-                if t % per_bank == 0:
-                    bank = psum.tile([P, BANK], F32, name="bank")
-                result = bank[:, (t % per_bank) * width : (t % per_bank + 1) * width]
-                multiply_mx(result, w_codes, w_plane, t, codes, plane)
-                results.append(result)
-            return results
-
         w1_codes = deal_words("w1_codes", w1_raw)
         picked_plane = sbuf("picked_plane", [P, S], U8)
         nc.vector.tensor_copy(picked_plane[:], x_plane[:].indirect(offs_sb[:]))
         picked = []
-        for start, width in spans(TOKEN_PIECES):
-            piece = sbuf("picked%d" % start, [P, width], U32, "w1_raw_plane" if start == TOKEN_PIECES[0] else "")
+        for start, width in TOKEN_PIECES:
+            if start == S // 2:
+                w1_plane = deal_plane("w1_plane", w1_raw_plane)
+            piece = sbuf("picked%d" % start, [P, width], U32, "w1_raw_plane" if start == S // 2 else None)
             nc.vector.tensor_copy(piece[:], x_table[:].indirect(entries(offs_sb, start, width)))
             picked.append(piece)
-            if start == 0:
-                w1_plane = deal_plane("w1_plane", w1_raw_plane)
         y = [sbuf("y%d" % t, [P, S], F32) for t in range(PACK)]
         for t in range(PACK):
-            for (start, width), piece in zip(spans(TOKEN_PIECES), picked):
+            for (start, width), piece in zip(TOKEN_PIECES, picked):
+                tokens = slice(start, start + width)
                 bank = psum.tile([P, BANK], F32, name="bank")
-                multiply_mx(bank[:, :width], w1_codes, w1_plane, t, piece[:], picked_plane[:, start : start + width])
-                nc.scalar.copy(y[t][:, start : start + width], bank[:, :width])
+                multiply_mx(bank[:, :width], w1_codes, w1_plane, t, piece[:], picked_plane[:, tokens])
+                nc.scalar.copy(y[t][:, tokens], bank[:, :width])
         w2_codes = deal_words("w2_codes", w2_raw)
         w2_plane = deal_plane("w2_plane", w2_raw_plane)
-
-        half_h = [sbuf("half_h%d" % t, [P, V], F32) for t in range(PACK)]
-        h = sbuf("h", [P, PACK, V], F32)
 
         lined = sbuf("lined", [P, PACK, S], F32)
         smaller = sbuf("smaller", [P, PACK, V], F32)
         larger = sbuf("larger", [P, PACK, V], F32)
         bent = sbuf("bent", [P, PACK, V], F32)
         gained = sbuf("gained", [P, PACK, V], F32)
-        halves = [slice(0, V // 2), slice(V // 2, V)]
-        for t in range(PACK):
-            for half in halves:
-                nc.vector.tensor_copy(
-                    lined[:, t, 2 * half.start : 2 * half.stop],
-                    y[t][:].indirect(entries(order_sb, 2 * half.start, V)),
-                )
-            for half in halves:
-                first = lined[:, t, 2 * half.start : 2 * half.stop : 2]
-                second = lined[:, t, 2 * half.start + 1 : 2 * half.stop : 2]
-                nc.vector.tensor_tensor(smaller[:, t, half], first, second, ALU.min)
-                nc.vector.tensor_tensor(larger[:, t, half], first, second, ALU.max)
-                nc.scalar.activation(bent[:, t, half], smaller[:, t, half], ACT.Tanh)
-                nc.scalar.activation(gained[:, t, half], larger[:, t, half], ACT.Copy, scale=gain[:, t : t + 1])
+        minus_half_h = [sbuf("minus_half_h%d" % t, [P, V], F32) for t in range(PACK)]
+        h = sbuf("h", [P, PACK, V], F32)
 
-        def multiply(start, width):
-            cols = slice(start, start + width)
+        def line_up(t, start, width):
+            pairs = slice(2 * start, 2 * (start + width))
+            nc.vector.tensor_copy(lined[:, t, pairs], y[t][:].indirect(entries(order_sb, 2 * start, 2 * width)))
+
+        def pool(t, start, width):
+            places = slice(start, start + width)
+            first = lined[:, t, 2 * start : 2 * (start + width) : 2]
+            second = lined[:, t, 2 * start + 1 : 2 * (start + width) : 2]
+            nc.vector.tensor_tensor(smaller[:, t, places], first, second, ALU.min)
+            nc.vector.tensor_tensor(larger[:, t, places], first, second, ALU.max)
+            nc.scalar.activation(bent[:, t, places], smaller[:, t, places], ACT.Tanh)
+            nc.scalar.activation(gained[:, t, places], larger[:, t, places], ACT.Copy, scale=gain[:, t : t + 1])
+
+        def make_z(start, width):
+            places = slice(start, start + width)
             z = sbuf("z%d" % start, [P, width * PACK], BF16)
-            nc.vector.tensor_tensor(by_column(z[:]), in_pairs(gained[:, :, cols]), in_pairs(bent[:, :, cols]), ALU.mult)
+            nc.vector.tensor_tensor(
+                side_by_side(z[:]), from_tiles(gained[:, :, places]), from_tiles(bent[:, :, places]), ALU.mult
+            )
             return z
 
-        def second_product(start, width, z):
+        def quantise_z(start, width, z):
             z_codes = sbuf("z_codes%d" % start, [P, width], U32)
             z_plane = sbuf("z_plane%d" % start, [P, width], U8)
             nc.vector.quantize_mx(out=z_codes[:].bitcast(FP8X4), scales=z_plane[:], in_=z[:])
-            return product(w2_codes, w2_plane, z_codes[:], z_plane[:], width)
+            return z_codes, z_plane
 
-        waiting = None
-        h_psum = []
-        for start, width in spans(POOL_PIECES):
-            z = multiply(start, width)
-            if waiting is not None:
-                h_psum.append(second_product(*waiting))
-            waiting = (start, width, z)
-        h_psum.append(second_product(*waiting))
-        pieces = list(zip(spans(POOL_PIECES), h_psum))
+        def make_h(t, start, width, z_codes, z_plane):
+            bank = psum.tile([P, BANK], F32, name="bank")
+            multiply_mx(bank[:, :width], w2_codes, w2_plane, t, z_codes[:], z_plane[:])
+            nc.scalar.mul(minus_half_h[t][:, start : start + width], bank[:, :width], -0.5)
+            return bank[:, :width]
+
+        for t in (0, 1):
+            line_up(t, *FIRST_HALF)
+            line_up(t, *SECOND_HALF)
+            pool(t, *FIRST_HALF)
+            pool(t, *SECOND_HALF)
+        for t in (2, 3):
+            line_up(t, *FIRST_HALF)
+        for t in (2, 3):
+            pool(t, *FIRST_HALF)
+        line_up(2, *SECOND_HALF)
+        z_first = make_z(*FIRST_HALF)
+        line_up(3, *SECOND_HALF)
+        operand_first = quantise_z(*FIRST_HALF, z_first)
         for t in range(PACK):
-            (start, width), results = pieces[0]
-            nc.scalar.copy(h[:, t, start : start + width], results[t])
-            for (start, width), results in pieces:
-                nc.scalar.mul(half_h[t][:, start : start + width], results[t], -0.5)
-        for (start, width), results in pieces[1:]:
+            nc.scalar.copy(h[:, t, : V // 2], make_h(t, *FIRST_HALF, *operand_first))
+        pool(2, *SECOND_HALF)
+        for quarter in LAST_QUARTERS:
+            pool(3, *quarter)
+        z_last = [make_z(*quarter) for quarter in LAST_QUARTERS]
+        operands_last = [quantise_z(*quarter, z) for quarter, z in zip(LAST_QUARTERS, z_last)]
+        h_last = [
+            [make_h(t, *quarter, *operand) for quarter, operand in zip(LAST_QUARTERS, operands_last)]
+            for t in range(PACK)
+        ]
+        for number, (start, width) in enumerate(LAST_QUARTERS):
             for t in range(PACK):
-                nc.scalar.copy(h[:, t, start : start + width], results[t])
+                nc.scalar.copy(h[:, t, start : start + width], h_last[t][number])
 
         out_rows = out_0.rearrange("(p t) v -> p t v", t=PACK)
         out_words = words_of(out_1)
         out_plane = sbuf("out_plane", [P, V], U8)
 
-        def store_rows(start, width, result):
-            nc.sync.dma_start(out_rows[:, :, start : start + width], result.rearrange("p (t v) -> p t v", t=PACK))
-
-        def neighbours(start, width):
+        def add_neighbours(start, width):
             last = start + width == V
-            partial = sbuf("partial%d" % start, [P, PACK * width], F32, "first_rounded" if last else "")
-            result = sbuf("result%d" % start, [P, PACK * width], F32)
-            for pair in range(0, PACK, 2):
-                for t in (pair, pair + 1):
-                    nc.vector.tensor_tensor(
-                        partial[:, t * width : (t + 1) * width],
-                        half_h[t][:].indirect(entries(n1_sb, start, width)),
-                        h[:, t, start : start + width],
-                        ALU.add,
-                    )
-                for t in (pair, pair + 1):
-                    nc.vector.tensor_tensor(
-                        result[:, t * width : (t + 1) * width],
-                        half_h[t][:].indirect(entries(n2_sb, start, width)),
-                        partial[:, t * width : (t + 1) * width],
-                        ALU.add,
-                    )
-            store_rows(start, width, result[:])
-            rounded = sbuf("rounded%d" % start, [P, width * PACK], BF16, "first_rounded" if start == 0 else "")
+            partial = sbuf("partial%d" % start, [P, PACK, width], F32, "rounded0" if last else None)
+            result = sbuf("result%d" % start, [P, PACK, width], F32)
+            for pair in ((0, 1), (2, 3)):
+                for t in pair:
+                    fetched = minus_half_h[t][:].indirect(entries(n1_sb, start, width))
+                    nc.vector.tensor_tensor(partial[:, t, :], fetched, h[:, t, start : start + width], ALU.add)
+                for t in pair:
+                    fetched = minus_half_h[t][:].indirect(entries(n2_sb, start, width))
+                    nc.vector.tensor_tensor(result[:, t, :], fetched, partial[:, t, :], ALU.add)
+            nc.sync.dma_start(out_rows[:, :, start : start + width], result[:])
+            rounded = sbuf("rounded%d" % start, [P, width * PACK], BF16)
             if last:
-                nc.vector.tensor_copy(by_column(rounded[:]), by_plane(result[:]))
+                nc.vector.tensor_copy(side_by_side(rounded[:]), from_tiles(result[:]))
             else:
-                nc.scalar.copy(by_column(rounded[:]), by_plane(result[:]))
+                nc.scalar.copy(side_by_side(rounded[:]), from_tiles(result[:]))
             return rounded
 
-        def planes(start, width, rounded):
+        def quantise_out(start, width, rounded):
+            places = slice(start, start + width)
             codes = sbuf("codes%d" % start, [P, width], U32)
-            nc.vector.quantize_mx(
-                out=codes[:].bitcast(FP8X4), scales=out_plane[:, start : start + width], in_=rounded[:]
-            )
-            nc.sync.dma_start(out_words[:, start : start + width], codes[:].bitcast(I32))
+            nc.vector.quantize_mx(out=codes[:].bitcast(FP8X4), scales=out_plane[:, places], in_=rounded[:])
+            nc.sync.dma_start(out_words[:, places], codes[:].bitcast(I32))
 
-        waiting = None
-        for start, width in spans(OUT_PIECES):
-            rounded = neighbours(start, width)
-            if waiting is not None:
-                planes(*waiting)
-            waiting = (start, width, rounded)
-        planes(*waiting)
+        made = None
+        for start, width in (FIRST_HALF,) + LAST_QUARTERS:
+            rounded = add_neighbours(start, width)
+            if made is not None:
+                quantise_out(*made)
+            made = (start, width, rounded)
+        quantise_out(*made)
+
         scale_rows = out_2[0].bitcast(I32)
-        for q in range(QUADS):
+        for q in range(QUADRANTS):
             queue = nc.scalar if q % 2 else nc.sync
             queue.dma_start(scale_rows[4 * q : 4 * q + 4, :], out_plane[32 * q : 32 * q + 4, :].bitcast(I32))

from contextlib import ExitStack

import concourse.mybir as mybir

K, T, S, V, N, H = 512, 2048, 1024, 512, 512, 512
FLOPS = 2 * K * H * S + 2 * H * N * V

F32 = mybir.dt.float32
BF16 = mybir.dt.bfloat16
I32 = mybir.dt.int32
U32 = mybir.dt.uint32
U16 = mybir.dt.uint16
U8 = mybir.dt.uint8
FP8X4 = mybir.dt.float8_e4m3fn_x4
ALU = mybir.AluOpType
ACT = mybir.ActivationFunctionType

P = 128
PACK = 4
STRIPE = 16
QUADRANTS = 4
BANK = 512

TOKEN_PIECES = ((0, 512), (512, 256), (768, 256))
FIRST_HALF, SECOND_HALF = (0, V // 2), (V // 2, V // 2)
LAST_QUARTERS = ((V // 2, V // 4), (3 * V // 4, V // 4))


def entries(list_tile, start, count):
    return list_tile[:, start // STRIPE : (start + count) // STRIPE]


def words_of(dram):
    return dram[0].rearrange("p n t -> p (n t)").bitcast(I32)


def load_scale_rows(nc, plane, dram):
    rows = dram[0].bitcast(I32)
    for q in range(QUADRANTS):
        nc.sync.dma_start(plane[32 * q : 32 * q + 4, :].bitcast(I32), rows[4 * q : 4 * q + 4, :])


def from_tiles(values):
    return values.rearrange("p t (c i) -> p c t i", i=2)


def side_by_side(flat):
    return flat.rearrange("p (c i t) -> p c t i", t=PACK, i=2)


def tile_picked_prodpool_none_po_kernel(
    tc, x_words, x_scales, w1_words, w1_scales, gn, w2_words, w2_scales, offs, order, n1, n2, out_0, out_1, out_2
):
    nc = tc.nc
    with ExitStack() as ctx:
        keep = ctx.enter_context(tc.tile_pool(name="keep", bufs=1))
        psum = ctx.enter_context(tc.psum_pool(name="psum", bufs=8))

        def sbuf(name, shape, dtype, reuses=None):
            return keep.tile(shape, dtype, name=name, tag=reuses or name, align_bytes=64)

        offs_sb = sbuf("offs_sb", [P, S // STRIPE], U16)
        order_sb = sbuf("order_sb", [P, S // STRIPE], U16)
        n1_sb = sbuf("n1_sb", [P, V // STRIPE], U16)
        n2_sb = sbuf("n2_sb", [P, V // STRIPE], U16)
        x_table = sbuf("x_table", [P, T], U32)
        x_plane = sbuf("x_plane", [P, T], U8)
        w1_raw = sbuf("w1_raw", [P, H], I32)
        w2_raw = sbuf("w2_raw", [P, N], I32)
        w1_raw_plane = sbuf("w1_raw_plane", [P, H], U8)
        w2_raw_plane = sbuf("w2_raw_plane", [P, N], U8)
        gain = sbuf("gain", [P, PACK], F32)

        nc.vector.memset(x_plane[:].bitcast(I32), 0)
        nc.gpsimd.memset(w1_raw_plane[:].bitcast(I32), 0)
        nc.gpsimd.memset(w2_raw_plane[:].bitcast(I32), 0)

        nc.sync.dma_start(offs_sb[:], offs)
        nc.sync.dma_start(w1_raw[:], words_of(w1_words))
        load_scale_rows(nc, x_plane, x_scales)
        nc.sync.dma_start(x_table[:].bitcast(I32), words_of(x_words))
        load_scale_rows(nc, w1_raw_plane, w1_scales)
        nc.sync.dma_start(order_sb[:], order)
        nc.sync.dma_start(w2_raw[:], words_of(w2_words))
        load_scale_rows(nc, w2_raw_plane, w2_scales)
        nc.sync.dma_start(gain[:], gn.rearrange("(p t) o -> p (t o)", t=PACK))
        nc.sync.dma_start(n1_sb[:], n1)
        nc.sync.dma_start(n2_sb[:], n2)

        def deal_words(name, raw):
            dealt = sbuf(name, [P, PACK * P], U32)
            nc.vector.tensor_copy(
                dealt[:].bitcast(I32).rearrange("p (t c i) -> p c t i", t=PACK, i=4),
                raw[:].rearrange("p (c i t) -> p c t i", t=PACK, i=4),
            )
            return dealt

        def deal_plane(name, raw):
            dealt = sbuf(name, [P, PACK * P], U8)
            nc.vector.tensor_copy(
                dealt[:].rearrange("p (t m) -> p t m", t=PACK), raw[:].rearrange("p (m t) -> p t m", t=PACK)
            )
            return dealt

        def multiply_mx(result, w_codes, w_plane, t, codes, plane):
            nc.tensor.matmul_mx(
                out=result,
                lhsT=w_codes[:, t * P : (t + 1) * P].bitcast(FP8X4),
                lhsT_scale=w_plane[:, t * P : (t + 1) * P],
                rhs=codes.bitcast(FP8X4),
                rhs_scale=plane,
                start=True,
                stop=True,
            )

        w1_codes = deal_words("w1_codes", w1_raw)
        picked_plane = sbuf("picked_plane", [P, S], U8)
        nc.vector.tensor_copy(picked_plane[:], x_plane[:].indirect(offs_sb[:]))
        picked = []
        for start, width in TOKEN_PIECES:
            if start == S // 2:
                w1_plane = deal_plane("w1_plane", w1_raw_plane)
            piece = sbuf("picked%d" % start, [P, width], U32, "w1_raw_plane" if start == S // 2 else None)
            nc.vector.tensor_copy(piece[:], x_table[:].indirect(entries(offs_sb, start, width)))
            picked.append(piece)
        y = [sbuf("y%d" % t, [P, S], F32) for t in range(PACK)]
        for t in range(PACK):
            for (start, width), piece in zip(TOKEN_PIECES, picked):
                tokens = slice(start, start + width)
                bank = psum.tile([P, BANK], F32, name="bank")
                multiply_mx(bank[:, :width], w1_codes, w1_plane, t, piece[:], picked_plane[:, tokens])
                nc.scalar.copy(y[t][:, tokens], bank[:, :width])
        w2_codes = deal_words("w2_codes", w2_raw)
        w2_plane = deal_plane("w2_plane", w2_raw_plane)

        lined = sbuf("lined", [P, PACK, S], F32)
        smaller = sbuf("smaller", [P, PACK, V], F32)
        larger = sbuf("larger", [P, PACK, V], F32)
        bent = sbuf("bent", [P, PACK, V], F32)
        gained = sbuf("gained", [P, PACK, V], F32)
        minus_half_h = [sbuf("minus_half_h%d" % t, [P, V], F32) for t in range(PACK)]
        h = sbuf("h", [P, PACK, V], F32)

        def line_up(t, start, width):
            pairs = slice(2 * start, 2 * (start + width))
            nc.vector.tensor_copy(lined[:, t, pairs], y[t][:].indirect(entries(order_sb, 2 * start, 2 * width)))

        def pool(t, start, width):
            places = slice(start, start + width)
            first = lined[:, t, 2 * start : 2 * (start + width) : 2]
            second = lined[:, t, 2 * start + 1 : 2 * (start + width) : 2]
            nc.vector.tensor_tensor(smaller[:, t, places], first, second, ALU.min)
            nc.vector.tensor_tensor(larger[:, t, places], first, second, ALU.max)
            nc.scalar.activation(bent[:, t, places], smaller[:, t, places], ACT.Tanh)
            nc.scalar.activation(gained[:, t, places], larger[:, t, places], ACT.Copy, scale=gain[:, t : t + 1])

        def make_z(start, width):
            places = slice(start, start + width)
            z = sbuf("z%d" % start, [P, width * PACK], BF16)
            nc.vector.tensor_tensor(
                side_by_side(z[:]), from_tiles(gained[:, :, places]), from_tiles(bent[:, :, places]), ALU.mult
            )
            return z

        def quantise_z(start, width, z):
            z_codes = sbuf("z_codes%d" % start, [P, width], U32)
            z_plane = sbuf("z_plane%d" % start, [P, width], U8)
            nc.vector.quantize_mx(out=z_codes[:].bitcast(FP8X4), scales=z_plane[:], in_=z[:])
            return z_codes, z_plane

        def make_h(t, start, width, z_codes, z_plane):
            bank = psum.tile([P, BANK], F32, name="bank")
            multiply_mx(bank[:, :width], w2_codes, w2_plane, t, z_codes[:], z_plane[:])
            nc.scalar.mul(minus_half_h[t][:, start : start + width], bank[:, :width], -0.5)
            return bank[:, :width]

        for t in (0, 1):
            line_up(t, *FIRST_HALF)
            line_up(t, *SECOND_HALF)
            pool(t, *FIRST_HALF)
            pool(t, *SECOND_HALF)
        for t in (2, 3):
            line_up(t, *FIRST_HALF)
        for t in (2, 3):
            pool(t, *FIRST_HALF)
        line_up(2, *SECOND_HALF)
        z_first = make_z(*FIRST_HALF)
        line_up(3, *SECOND_HALF)
        operand_first = quantise_z(*FIRST_HALF, z_first)
        for t in range(PACK):
            nc.scalar.copy(h[:, t, : V // 2], make_h(t, *FIRST_HALF, *operand_first))
        pool(2, *SECOND_HALF)
        for quarter in LAST_QUARTERS:
            pool(3, *quarter)
        z_last = [make_z(*quarter) for quarter in LAST_QUARTERS]
        operands_last = [quantise_z(*quarter, z) for quarter, z in zip(LAST_QUARTERS, z_last)]
        h_last = [
            [make_h(t, *quarter, *operand) for quarter, operand in zip(LAST_QUARTERS, operands_last)]
            for t in range(PACK)
        ]
        for number, (start, width) in enumerate(LAST_QUARTERS):
            for t in range(PACK):
                nc.scalar.copy(h[:, t, start : start + width], h_last[t][number])

        out_rows = out_0.rearrange("(p t) v -> p t v", t=PACK)
        out_words = words_of(out_1)
        out_plane = sbuf("out_plane", [P, V], U8)

        def add_neighbours(start, width):
            last = start + width == V
            partial = sbuf("partial%d" % start, [P, PACK, width], F32, "rounded0" if last else None)
            result = sbuf("result%d" % start, [P, PACK, width], F32)
            for pair in ((0, 1), (2, 3)):
                for t in pair:
                    fetched = minus_half_h[t][:].indirect(entries(n1_sb, start, width))
                    nc.vector.tensor_tensor(partial[:, t, :], fetched, h[:, t, start : start + width], ALU.add)
                for t in pair:
                    fetched = minus_half_h[t][:].indirect(entries(n2_sb, start, width))
                    nc.vector.tensor_tensor(result[:, t, :], fetched, partial[:, t, :], ALU.add)
            nc.sync.dma_start(out_rows[:, :, start : start + width], result[:])
            rounded = sbuf("rounded%d" % start, [P, width * PACK], BF16)
            if last:
                nc.vector.tensor_copy(side_by_side(rounded[:]), from_tiles(result[:]))
            else:
                nc.scalar.copy(side_by_side(rounded[:]), from_tiles(result[:]))
            return rounded

        def quantise_out(start, width, rounded):
            places = slice(start, start + width)
            codes = sbuf("codes%d" % start, [P, width], U32)
            nc.vector.quantize_mx(out=codes[:].bitcast(FP8X4), scales=out_plane[:, places], in_=rounded[:])
            nc.sync.dma_start(out_words[:, places], codes[:].bitcast(I32))

        made = None
        for start, width in (FIRST_HALF,) + LAST_QUARTERS:
            rounded = add_neighbours(start, width)
            if made is not None:
                quantise_out(*made)
            made = (start, width, rounded)
        quantise_out(*made)

        scale_rows = out_2[0].bitcast(I32)
        for q in range(QUADRANTS):
            queue = nc.scalar if q % 2 else nc.sync
            queue.dma_start(scale_rows[4 * q : 4 * q + 4, :], out_plane[32 * q : 32 * q + 4, :].bitcast(I32))
